import numpy as np
import ml_dtypes


def mxq(x, axis, fmt="e4m3"):
    dtype, down = {"e4m3": (ml_dtypes.float8_e4m3fn, 7), "e5m2": (ml_dtypes.float8_e5m2, 14)}[fmt]
    v = np.moveaxis(np.asarray(x, np.float32).astype(ml_dtypes.bfloat16).astype(np.float64), axis, -1)
    blocks = v.reshape(v.shape[:-1] + (-1, 32))
    amax = np.abs(blocks).max(-1, keepdims=True)
    byte = np.maximum(np.where(amax > 0, np.frexp(amax)[1] - 1 + 127, 0) - down, 1)
    scale = np.exp2(byte - 127.0)
    codes = (blocks / scale).astype(np.float32).astype(dtype).astype(np.float64)
    return np.moveaxis((codes * scale).reshape(v.shape), -1, axis)


WIDE = False


def mx_kscale(k):
    if not WIDE:
        return np.ones(k)
    levels = np.array([10, -10, 5, -5, 0])
    if k % 512:
        return np.exp2(np.random.permutation(np.resize(levels, k // 32))).repeat(32)
    a = np.empty((k // 512, 16))
    for p in range(k // 512):
        a[p, :8] = np.random.permutation(np.resize(levels, 8))
        for g in range(8):
            far = levels[np.abs(levels - a[p, g]) >= 10]
            a[p, g + 8] = far[np.random.randint(len(far))]
    return np.exp2(a.ravel()).repeat(32)


BF16 = ml_dtypes.bfloat16


def bf(x):
    return np.asarray(x, np.float32).astype(BF16)


def f64(x):
    return np.asarray(x).astype(np.float64)


E2M1 = np.array([0.0, 0.5, 1.0, 1.5, 2.0, 3.0, 4.0, 6.0, -0.0, -0.5, -1.0, -1.5, -2.0, -3.0, -4.0, -6.0])


def pack_weight(w, fmt):
    k, n = w.shape
    w = f64(bf(w)).reshape(k // 32, 32, n)
    amax = np.abs(w).max(1)
    if fmt == "e4m3":
        byte = np.frexp(amax)[1] - 1 + 127 - 7
    else:
        mant, ex = np.frexp(amax / 6.0)
        byte = np.where(mant > 0.5, ex, ex - 1) + 127
    byte = np.clip(np.where(amax > 0, byte, 1), 1, 254)
    scaled = (w * np.exp2(127.0 - byte)[:, None, :]).reshape(k, n).astype(np.float32)
    by_word = np.ascontiguousarray(scaled.reshape(k // 512, 128, 4, n).transpose(0, 1, 3, 2))
    if fmt == "e4m3":
        words = by_word.astype(ml_dtypes.float8_e4m3fn).view(np.uint8)
    else:
        c = by_word.astype(ml_dtypes.float4_e2m1fn).view(np.uint8) & 0xF
        words = c[..., 0::2] | (c[..., 1::2] << 4)
    return np.ascontiguousarray(words), np.ascontiguousarray(byte.astype(np.uint8).reshape(k // 512, 16, n))


def unpack_weight(words, scales, fmt):
    g, p, n, _ = words.shape
    if fmt == "e4m3":
        vals = np.ascontiguousarray(words).view(ml_dtypes.float8_e4m3fn).astype(np.float64)
    else:
        nib = np.empty((g, p, n, 4), np.uint8)
        nib[..., 0::2] = words & 0xF
        nib[..., 1::2] = words >> 4
        vals = E2M1[nib]
    vals = vals * np.repeat(np.exp2(scales.astype(np.float64) - 127.0), 8, axis=1)[..., None]
    return vals.transpose(0, 1, 3, 2).reshape(g * 512, n)


N, D, K = 2048, 1024, 512


def scale_rows(gain, m):
    return gain[:, None] * m


def draw0():
    s = mx_kscale(D)
    u = mx_kscale(N)
    x = bf(np.random.standard_normal((N, D)) * s)
    p_words, p_scales = pack_weight(np.random.standard_normal((D, D)) / np.sqrt(D) / s[:, None], "e4m3")
    beta_words, beta_scales = pack_weight(np.random.standard_normal((D, K)) / np.sqrt(D) / s[:, None], "e4m3")
    return {
        "x": x,
        "p_words": p_words,
        "p_scales": p_scales,
        "beta_words": beta_words,
        "beta_scales": beta_scales,
        "r": bf(np.random.uniform(0.5, 1.5, N) * u),
        "t": bf((1.0 + 0.3 * np.random.standard_normal(N)) / u),
        "v": bf(np.random.standard_normal((D, K)) / np.sqrt(D)),
        "psi": bf(np.random.uniform(0.05, 0.2, D)),
    }


def core(x, p_words, p_scales, beta_words, beta_scales, r, t, v, psi):
    n_cases = x.shape[0]
    xq = mxq(f64(x), 1, "e4m3")
    e0 = xq @ unpack_weight(p_words, p_scales, "e4m3")
    e = scale_rows(f64(r), e0)
    z0 = xq @ unpack_weight(beta_words, beta_scales, "e4m3")
    z = scale_rows(f64(t), z0)
    c = mxq(e, 0, "e4m3").T @ mxq(z, 0, "e4m3")
    return (c / n_cases - f64(v)) / f64(psi)[:, None]


def e4m3fn_bytes(y):
    return np.clip(np.asarray(y, np.float64), -448.0, 448.0).astype(np.float32).astype(ml_dtypes.float8_e4m3fn).view(np.uint8)


def e4m3fn_values(b):
    return np.asarray(b, np.uint8).view(ml_dtypes.float8_e4m3fn).astype(np.float64)


def setup_inputs():
    d = draw0()
    x0 = np.asarray(d['x']).astype(np.float64)
    s = (np.max(np.abs(x0), axis=(0,), keepdims=True) / 448.0).astype(np.float32)
    out = {}
    for k, v in d.items():
        if k == 'x':
            out['x_bytes'] = e4m3fn_bytes(x0 / s.astype(np.float64))
            out['x_scale'] = s
        else:
            out[k] = v
    return out


def reference(x_bytes, x_scale, p_words, p_scales, beta_words, beta_scales, r, t, v, psi):
    return core(e4m3fn_values(x_bytes) * x_scale.astype(np.float64), p_words, p_scales, beta_words, beta_scales, r, t, v, psi)

@@ -1,0 +1,311 @@
+from contextlib import ExitStack
+
+import concourse.mybir as mybir
+from concourse.masks import make_identity
+
+N, D, K = 2048, 1024, 512
+FLOPS = 2 * N * D * (D + K) + 2 * N * D * K
+
+F32 = mybir.dt.float32
+BF16 = mybir.dt.bfloat16
+U32 = mybir.dt.uint32
+I32 = mybir.dt.int32
+U8 = mybir.dt.uint8
+FP8 = mybir.dt.float8_e4m3fn
+X4 = mybir.dt.float8_e4m3fn_x4
+MULT = mybir.AluOpType.mult
+SUB = mybir.AluOpType.subtract
+COPY = mybir.ActivationFunctionType.Copy
+
+ENG = mybir.EngineType
+
+P = 128
+T = 4
+G = N // (P * T)
+J = D // (P * T)
+HALF = D // 2
+
+
+def tile_factoranalysisemloadinggradient_w8_kernel(
+    tc, x_bytes, x_scale, p_words, p_scales, beta_words, beta_scales, r, t, v, psi, out
+):
+    nc = tc.nc
+    with ExitStack() as ctx:
+        keep = ctx.enter_context(tc.tile_pool(name="keep", bufs=1))
+        work = ctx.enter_context(tc.tile_pool(name="work", bufs=4))
+        xps = ctx.enter_context(tc.psum_pool(name="xps", bufs=2))
+        aps = ctx.enter_context(tc.psum_pool(name="aps", bufs=6))
+
+        x_in = x_bytes.rearrange("(g p t) k -> g p t k", p=P, t=T)
+        sc = keep.tile([P, D], F32, name="sc")
+        for h in range(2):
+            cols = slice(h * HALF, (h + 1) * HALF)
+            nc.scalar.dma_start(
+                out=sc[:, cols], in_=x_scale.rearrange("o k -> (o k)")[cols].partition_broadcast(P)
+            )
+        xb = []
+        for s in range(2 * G):
+            xb.append(keep.tile([P, 2, D], U8, name="xb%d" % s))
+
+        def load_x(s):
+            g, h = divmod(s, 2)
+            nc.sync.dma_start(out=xb[s][:], in_=x_in[g][:, 2 * h : 2 * h + 2, :])
+
+        for i in range(2):
+            nc.sync.dma_start(out=xb[0][:, i : i + 1, :], in_=x_in[0][:, i : i + 1, :])
+
+        ws = keep.tile([P, D + K], U8, name="ws", align_bytes=64)
+        nc.vector.memset(ws[:].bitcast(I32), 0)
+        ident = keep.tile([P, P], F32, name="ident")
+        make_identity(nc, ident[:])
+
+        wb = keep.tile([P, J, K * T], U8, name="wb", align_bytes=64)
+        wp = []
+        for h in range(2):
+            wp.append(keep.tile([P, J, HALF * T], U8, name="wp%d" % h, align_bytes=64))
+        load_x(1)
+        nc.sync.dma_start(out=wb[:], in_=beta_words.rearrange("g p n t -> p g (n t)"))
+        ps32 = p_scales.bitcast(I32)
+        bs32 = beta_scales.bitcast(I32)
+        for q in range(4):
+            rows = slice(32 * q, 32 * q + 8)
+            nc.sync.dma_start(out=ws[rows, D : D + K].bitcast(I32), in_=bs32[:, 4 * q : 4 * q + 4, :])
+        for q in range(4):
+            rows = slice(32 * q, 32 * q + 8)
+            nc.sync.dma_start(out=ws[rows, 0:D].bitcast(I32), in_=ps32[:, 4 * q : 4 * q + 4, :])
+        pw = p_words.rearrange("g p n t -> p g (n t)")
+        nc.sync.dma_start(out=wp[0][:], in_=pw[:, :, 0 : HALF * T])
+        load_x(2)
+        nc.sync.dma_start(out=wp[1][:], in_=pw[:, :, HALF * T : D * T])
+        for s in range(3, 2 * G):
+            load_x(s)
+
+        rt_in = keep.tile([P, 2, G, T], BF16, name="rt_in")
+        rt = keep.tile([P, 2, G * T], F32, name="rt")
+        psi_in = keep.tile([P, D // P, 2], BF16, name="psi_in")
+        v_in = keep.tile([P, D // P, K], BF16, name="v_in")
+        with nc.allow_non_contiguous_dma(reason="small vectors laid on the partitions"):
+            nc.scalar.dma_start(out=rt_in[:, 0, :, :], in_=r.rearrange("(g p t) -> p g t", p=P, t=T))
+            nc.scalar.dma_start(out=rt_in[:, 1, :, :], in_=t.rearrange("(g p t) -> p g t", p=P, t=T))
+            nc.sync.dma_start(out=psi_in[:, :, 0:1], in_=psi.rearrange("(m p o) -> p m o", p=P, o=1))
+        nc.sync.dma_start(out=v_in[:], in_=v.rearrange("(m p) k -> p m k", p=P))
+
+        xs = {}
+        gx = {}
+        xc = []
+        xq = []
+        for i in range(G * T):
+            xc.append(keep.tile([P, J * P], U32, name="xc%d" % i, align_bytes=64))
+            xq.append(keep.tile([P, J * P], U8, name="xq%d" % i, align_bytes=64))
+        zc, zq, ec, eq = [], [], [], []
+        for g in range(G):
+            zc.append(keep.tile([P, K], U32, name="zc%d" % g, align_bytes=64))
+            zq.append(keep.tile([P, K], U8, name="zq%d" % g, align_bytes=64))
+            ec.append(keep.tile([P, D], U32, name="ec%d" % g, align_bytes=64))
+            eq.append(keep.tile([P, D], U8, name="eq%d" % g, align_bytes=64))
+
+        def product(i):
+            s, h = divmod(i, 2)
+            xs[i] = work.tile([P, D], BF16, name="xs")
+            if i == 0:
+                parts = 2
+            else:
+                parts = 1
+            w = D // parts
+            for n in range(parts):
+                cols = slice(n * w, (n + 1) * w)
+                nc.vector.tensor_tensor(
+                    out=xs[i][:, cols], in0=xb[s][:, h, cols].bitcast(FP8), in1=sc[:, cols], op=MULT
+                )
+
+        turned = {}
+
+        def turn(i):
+            words = xs[i][:].bitcast(F32)
+            xt = xps.tile([P, J, 2, P], F32, name="xt")
+            turned[i] = xt
+            for j in range(J):
+                for u in range(2):
+                    nc.tensor.transpose(
+                        xt[:, j, u, :], words[:, 256 * j + u : 256 * (j + 1) : 2], ident[:]
+                    )
+
+        def settle(i):
+            xt = turned[i]
+            gx[i] = work.tile([P, J * P * T], BF16, name="gx", align_bytes=64)
+            nc.scalar.copy(
+                out=gx[i][:].bitcast(F32).rearrange("p (j r u) -> p j r u", j=J, u=2),
+                in_=xt[:].rearrange("p j u r -> p j r u"),
+            )
+
+        def quant_x(i):
+            nc.vector.quantize_mx(out=xc[i][:].bitcast(X4), scales=xq[i][:], in_=gx[i][:])
+
+        def mx(acc, i, w_tile, w_word, s_col, width):
+            for j in range(J):
+                cols = slice(j * P, (j + 1) * P)
+                nc.tensor.matmul_mx(
+                    out=acc,
+                    lhsT=xc[i][:, cols].bitcast(X4),
+                    lhsT_scale=xq[i][:, cols],
+                    rhs=w_tile[:, j, w_word * T : (w_word + width) * T].bitcast(X4),
+                    rhs_scale=ws[4 * j : P, s_col : s_col + width],
+                    start=(j == 0),
+                    stop=(j == J - 1),
+                )
+
+        planes = {}
+
+        def wide_pair(i):
+            g, ti = divmod(i, T)
+            if ti == 0:
+                planes["z", g] = keep.tile([P, T, K], BF16, name="zp%d" % g)
+                planes["e", g] = keep.tile([P, T, HALF], BF16, name="ep%d" % g)
+            acc_z = aps.tile([P, K], F32, name="acc")
+            mx(acc_z[:], i, wb, 0, D, K)
+            nc.scalar.activation(out=planes["z", g][:, ti, :], in_=acc_z[:], func=COPY, scale=rt[:, 1, i : i + 1])
+            acc_e = aps.tile([P, HALF], F32, name="acc")
+            mx(acc_e[:], i, wp[0], 0, 0, HALF)
+            nc.scalar.activation(out=planes["e", g][:, ti, :], in_=acc_e[:], func=COPY, scale=rt[:, 0, i : i + 1])
+
+        def weave(kind, g, lo, hi, eng):
+            if (kind, g, "i") not in planes:
+                planes[kind, g, "i"] = keep.tile([P, HALF, T], BF16, name="%si%d" % (kind, g), align_bytes=64)
+            o = planes[kind, g, "i"][:, lo:hi, :].rearrange("p (c i) t -> p c t i", i=4)
+            a = planes[kind, g][:, :, lo:hi].rearrange("p t (c i) -> p c t i", i=4)
+            if eng == "V":
+                nc.vector.tensor_copy(out=o, in_=a)
+            else:
+                nc.scalar.copy(out=o, in_=a)
+
+        def quant_wide(kind, g):
+            src = planes[kind, g, "i"][:].rearrange("p c t -> p (c t)")
+            if kind == "z":
+                nc.vector.quantize_mx(out=zc[g][:].bitcast(X4), scales=zq[g][:], in_=src)
+            else:
+                nc.vector.quantize_mx(
+                    out=ec[g][:, 0:HALF].bitcast(X4), scales=eq[g][:, 0:HALF], in_=src
+                )
+
+        narrow = {}
+
+        def narrow_mm(g, c):
+            acc = aps.tile([P, T, P], F32, name="acc")
+            for ti in range(T):
+                mx(acc[:, ti, :], g * T + ti, wp[1], P * c, HALF + P * c, P)
+            if c % 2 == 0:
+                narrow[g, c // 2] = work.tile([P, 2, P, T], BF16, name="en", align_bytes=64)
+            nc.vector.tensor_tensor(
+                out=narrow[g, c // 2][:, c % 2, :, :],
+                in0=acc[:].rearrange("p t d -> p d t"),
+                in1=rt[:, 0, g * T : (g + 1) * T].unsqueeze(1).to_broadcast([P, P, T]),
+                op=MULT,
+            )
+
+        def quant_narrow(g, h):
+            cols = slice(HALF + 2 * P * h, HALF + 2 * P * (h + 1))
+            nc.vector.quantize_mx(
+                out=ec[g][:, cols].bitcast(X4),
+                scales=eq[g][:, cols],
+                in_=narrow[g, h][:].rearrange("p b d t -> p (b d t)"),
+            )
+
+        ipsi = keep.tile([P, D // P], F32, name="ipsi")
+        gain = keep.tile([P, D // P], F32, name="gain")
+        vs = keep.tile([P, D // P, K], F32, name="vs")
+
+        def scaled_v(m):
+            nc.scalar.activation(out=vs[:, m, :], in_=v_in[:, m, :], func=COPY, scale=ipsi[:, m : m + 1])
+
+        def finish(m):
+            acc = aps.tile([P, K], F32, name="acc")
+            cols = slice(P * m, P * (m + 1))
+            for g in range(G):
+                nc.tensor.matmul_mx(
+                    out=acc[:],
+                    lhsT=ec[g][:, cols].bitcast(X4),
+                    lhsT_scale=eq[g][:, cols],
+                    rhs=zc[g][:].bitcast(X4),
+                    rhs_scale=zq[g][:],
+                    start=(g == 0),
+                    stop=(g == G - 1),
+                )
+            o = work.tile([P, K], F32, name="o")
+            nc.vector.scalar_tensor_tensor(
+                out=o[:], in0=acc[:], scalar=gain[:, m : m + 1], in1=vs[:, m, :], op0=MULT, op1=SUB
+            )
+            nc.sync.dma_start(out=out[cols, :], in_=o[:])
+
+        with tc.manual_schedule(engines={ENG.PE, ENG.Activation, ENG.DVE}):
+            product(0)
+            turn(0)
+            settle(0)
+            product(1)
+            turn(1)
+            settle(1)
+            nc.vector.tensor_copy(out=rt[:].rearrange("p w i -> p (w i)"), in_=rt_in[:].rearrange("p w g t -> p (w g t)"))
+            quant_x(0)
+            product(2)
+            quant_x(1)
+            product(3)
+            for s in range(2 * G):
+                g, h = divmod(s, 2)
+                if s + 1 < 2 * G:
+                    turn(2 * s + 2)
+                    turn(2 * s + 3)
+                    settle(2 * s + 2)
+                    settle(2 * s + 3)
+                wide_pair(2 * s)
+                wide_pair(2 * s + 1)
+                if g > 0:
+                    weave("z", g - 1, 256 * h, 256 * h + 256, "S")
+                if s >= 4:
+                    weave("e", 0, 128 * (s - 4), 128 * (s - 3), "S")
+                if s + 2 < 2 * G:
+                    product(2 * s + 4)
+                if s + 1 < 2 * G:
+                    quant_x(2 * s + 2)
+                if s + 2 < 2 * G:
+                    product(2 * s + 5)
+                if s + 1 < 2 * G:
+                    quant_x(2 * s + 3)
+                if g > 0:
+                    if h == 0 and g > 1:
+                        quant_wide("z", g - 2)
+                    narrow_mm(g - 1, 2 * h)
+                    narrow_mm(g - 1, 2 * h + 1)
+                    quant_narrow(g - 1, h)
+                if s == 4:
+                    nc.vector.reciprocal(out=ipsi[:], in_=psi_in[:, :, 0])
+                    nc.vector.tensor_scalar(out=gain[:], in0=ipsi[:], scalar1=1.0 / N, scalar2=None, op0=MULT)
+            g = G - 1
+            weave("z", g, 256, 512, "S")
+            weave("z", g, 0, 256, "V")
+            quant_wide("z", g - 1)
+            narrow_mm(g, 0)
+            quant_wide("z", g)
+            narrow_mm(g, 1)
+            scaled_v(4)
+            scaled_v(5)
+            weave("e", 1, 0, 512, "S")
+            quant_wide("e", 0)
+            quant_narrow(g, 0)
+            narrow_mm(g, 2)
+            narrow_mm(g, 3)
+            weave("e", 2, 0, 512, "V")
+            quant_narrow(g, 1)
+            finish(4)
+            scaled_v(6)
+            scaled_v(7)
+            weave("e", 3, 256, 512, "S")
+            finish(5)
+            weave("e", 3, 0, 256, "V")
+            quant_wide("e", 1)
+            finish(6)
+            quant_wide("e", 2)
+            quant_wide("e", 3)
+            finish(7)
+            for m in range(4):
+                scaled_v(m)
+            for m in range(4):
+                finish(m)

@@ -38,11 +38,8 @@ def tile_factoranalysisemloadinggradient_w8_kernel(
 
         x_in = x_bytes.rearrange("(g p t) k -> g p t k", p=P, t=T)
         sc = keep.tile([P, D], F32, name="sc")
-        for h in range(2):
-            cols = slice(h * HALF, (h + 1) * HALF)
-            nc.scalar.dma_start(
-                out=sc[:, cols], in_=x_scale.rearrange("o k -> (o k)")[cols].partition_broadcast(P)
-            )
+        scol = keep.tile([P, J, T], F32, name="scol")
+        nc.scalar.dma_start(out=scol[:], in_=x_scale.rearrange("o (j p t) -> p (o j) t", p=P, t=T))
         xb = []
         for s in range(2 * G):
             xb.append(keep.tile([P, 2, D], U8, name="xb%d" % s))
@@ -50,9 +47,6 @@ def tile_factoranalysisemloadinggradient_w8_kernel(
         def load_x(s):
             g, h = divmod(s, 2)
             nc.sync.dma_start(out=xb[s][:], in_=x_in[g][:, 2 * h : 2 * h + 2, :])
-
-        for i in range(2):
-            nc.sync.dma_start(out=xb[0][:, i : i + 1, :], in_=x_in[0][:, i : i + 1, :])
 
         ws = keep.tile([P, D + K], U8, name="ws", align_bytes=64)
         nc.vector.memset(ws[:].bitcast(I32), 0)
@@ -63,30 +57,34 @@ def tile_factoranalysisemloadinggradient_w8_kernel(
         wp = []
         for h in range(2):
             wp.append(keep.tile([P, J, HALF * T], U8, name="wp%d" % h, align_bytes=64))
-        load_x(1)
-        nc.sync.dma_start(out=wb[:], in_=beta_words.rearrange("g p n t -> p g (n t)"))
         ps32 = p_scales.bitcast(I32)
         bs32 = beta_scales.bitcast(I32)
-        for q in range(4):
-            rows = slice(32 * q, 32 * q + 8)
-            nc.sync.dma_start(out=ws[rows, D : D + K].bitcast(I32), in_=bs32[:, 4 * q : 4 * q + 4, :])
-        for q in range(4):
-            rows = slice(32 * q, 32 * q + 8)
-            nc.sync.dma_start(out=ws[rows, 0:D].bitcast(I32), in_=ps32[:, 4 * q : 4 * q + 4, :])
         pw = p_words.rearrange("g p n t -> p g (n t)")
-        nc.sync.dma_start(out=wp[0][:], in_=pw[:, :, 0 : HALF * T])
-        load_x(2)
-        nc.sync.dma_start(out=wp[1][:], in_=pw[:, :, HALF * T : D * T])
-        for s in range(3, 2 * G):
-            load_x(s)
-
         rt_in = keep.tile([P, 2, G, T], BF16, name="rt_in")
         rt = keep.tile([P, 2, G * T], F32, name="rt")
         psi_in = keep.tile([P, D // P, 2], BF16, name="psi_in")
         v_in = keep.tile([P, D // P, K], BF16, name="v_in")
+
+        for h in range(2):
+            nc.sync.dma_start(out=xb[0][:, h : h + 1, :], in_=x_in[0][:, h : h + 1, :])
+        for q in range(4):
+            rows = slice(32 * q, 32 * q + 8)
+            nc.sync.dma_start(out=ws[rows, D : D + K].bitcast(I32), in_=bs32[:, 4 * q : 4 * q + 4, :])
+        nc.sync.dma_start(out=wb[:], in_=beta_words.rearrange("g p n t -> p g (n t)"))
+        load_x(1)
+        nc.sync.dma_start(out=wp[0][:], in_=pw[:, :, 0 : HALF * T])
+        for q in range(4):
+            rows = slice(32 * q, 32 * q + 8)
+            nc.sync.dma_start(out=ws[rows, 0:D].bitcast(I32), in_=ps32[:, 4 * q : 4 * q + 4, :])
+        nc.sync.dma_start(out=sc[:], in_=x_scale.rearrange("o k -> (o k)").partition_broadcast(P))
         with nc.allow_non_contiguous_dma(reason="small vectors laid on the partitions"):
-            nc.scalar.dma_start(out=rt_in[:, 0, :, :], in_=r.rearrange("(g p t) -> p g t", p=P, t=T))
-            nc.scalar.dma_start(out=rt_in[:, 1, :, :], in_=t.rearrange("(g p t) -> p g t", p=P, t=T))
+            nc.gpsimd.dma_start(out=rt_in[:, 1, :, :], in_=t.rearrange("(g p t) -> p g t", p=P, t=T))
+            nc.gpsimd.dma_start(out=rt_in[:, 0, :, :], in_=r.rearrange("(g p t) -> p g t", p=P, t=T))
+        load_x(2)
+        nc.sync.dma_start(out=wp[1][:], in_=pw[:, :, HALF * T : D * T])
+        for s in range(3, 2 * G):
+            load_x(s)
+        with nc.allow_non_contiguous_dma(reason="small vectors laid on the partitions"):
             nc.sync.dma_start(out=psi_in[:, :, 0:1], in_=psi.rearrange("(m p o) -> p m o", p=P, o=1))
         nc.sync.dma_start(out=v_in[:], in_=v.rearrange("(m p) k -> p m k", p=P))
 
@@ -107,15 +105,26 @@ def tile_factoranalysisemloadinggradient_w8_kernel(
         def product(i):
             s, h = divmod(i, 2)
             xs[i] = work.tile([P, D], BF16, name="xs")
-            if i == 0:
-                parts = 2
-            else:
-                parts = 1
-            w = D // parts
-            for n in range(parts):
-                cols = slice(n * w, (n + 1) * w)
+            nc.vector.tensor_tensor(out=xs[i][:], in0=xb[s][:, h, :].bitcast(FP8), in1=sc[:], op=MULT)
+
+        def widen(i, eng):
+            s, h = divmod(i, 2)
+            xs[i] = work.tile([P, D], BF16, name="xs")
+            for j in range(J):
+                cols = slice(j * HALF, (j + 1) * HALF)
+                if eng == "V":
+                    nc.vector.tensor_copy(out=xs[i][:, cols], in_=xb[s][:, h, cols].bitcast(FP8))
+                else:
+                    nc.scalar.copy(out=xs[i][:, cols], in_=xb[s][:, h, cols].bitcast(FP8))
+
+        def late(i):
+            gx[i] = work.tile([P, J * P * T], BF16, name="gx", align_bytes=64)
+            for j in range(J):
                 nc.vector.tensor_tensor(
-                    out=xs[i][:, cols], in0=xb[s][:, h, cols].bitcast(FP8), in1=sc[:, cols], op=MULT
+                    out=gx[i][:, j * P * T : (j + 1) * P * T].rearrange("p (r u e) -> p r u e", u=2, e=2),
+                    in0=turned[i][:, j, :, :].bitcast(BF16).rearrange("p u (r e) -> p r u e", e=2),
+                    in1=scol[:, j, :].rearrange("p (u e) -> p u e", e=2).unsqueeze(1).to_broadcast([P, P, 2, 2]),
+                    op=MULT,
                 )
 
         turned = {}
@@ -156,17 +165,24 @@ def tile_factoranalysisemloadinggradient_w8_kernel(
 
         planes = {}
 
-        def wide_pair(i):
+        banks = {}
+
+        def mm_wide(kind, i):
+            acc = aps.tile([P, K], F32, name="acc")
+            banks[kind, i] = acc
+            if kind == "z":
+                mx(acc[:], i, wb, 0, D, K)
+            else:
+                mx(acc[:], i, wp[0], 0, 0, HALF)
+
+        def evac_wide(kind, i):
             g, ti = divmod(i, T)
             if ti == 0:
-                planes["z", g] = keep.tile([P, T, K], BF16, name="zp%d" % g)
-                planes["e", g] = keep.tile([P, T, HALF], BF16, name="ep%d" % g)
-            acc_z = aps.tile([P, K], F32, name="acc")
-            mx(acc_z[:], i, wb, 0, D, K)
-            nc.scalar.activation(out=planes["z", g][:, ti, :], in_=acc_z[:], func=COPY, scale=rt[:, 1, i : i + 1])
-            acc_e = aps.tile([P, HALF], F32, name="acc")
-            mx(acc_e[:], i, wp[0], 0, 0, HALF)
-            nc.scalar.activation(out=planes["e", g][:, ti, :], in_=acc_e[:], func=COPY, scale=rt[:, 0, i : i + 1])
+                planes[kind, g] = keep.tile([P, T, K], BF16, name="%sp%d" % (kind, g))
+            w = (0, 1)[kind == "z"]
+            nc.scalar.activation(
+                out=planes[kind, g][:, ti, :], in_=banks[kind, i][:], func=COPY, scale=rt[:, w, i : i + 1]
+            )
 
         def weave(kind, g, lo, hi, eng):
             if (kind, g, "i") not in planes:
@@ -193,6 +209,10 @@ def tile_factoranalysisemloadinggradient_w8_kernel(
             acc = aps.tile([P, T, P], F32, name="acc")
             for ti in range(T):
                 mx(acc[:, ti, :], g * T + ti, wp[1], P * c, HALF + P * c, P)
+            banks["n", g, c] = acc
+
+        def evac_narrow(g, c):
+            acc = banks["n", g, c]
             if c % 2 == 0:
                 narrow[g, c // 2] = work.tile([P, 2, P, T], BF16, name="en", align_bytes=64)
             nc.vector.tensor_tensor(
@@ -217,12 +237,14 @@ def tile_factoranalysisemloadinggradient_w8_kernel(
         def scaled_v(m):
             nc.scalar.activation(out=vs[:, m, :], in_=v_in[:, m, :], func=COPY, scale=ipsi[:, m : m + 1])
 
-        def finish(m):
-            acc = aps.tile([P, K], F32, name="acc")
+        def s2(m, groups):
+            if m not in banks:
+                acc_m = aps.tile([P, K], F32, name="acc")
+                banks[m] = acc_m
             cols = slice(P * m, P * (m + 1))
-            for g in range(G):
+            for g in groups:
                 nc.tensor.matmul_mx(
-                    out=acc[:],
+                    out=banks[m][:],
                     lhsT=ec[g][:, cols].bitcast(X4),
                     lhsT_scale=eq[g][:, cols],
                     rhs=zc[g][:].bitcast(X4),
@@ -230,82 +252,119 @@ def tile_factoranalysisemloadinggradient_w8_kernel(
                     start=(g == 0),
                     stop=(g == G - 1),
                 )
+
+        def epi(m):
+            cols = slice(P * m, P * (m + 1))
             o = work.tile([P, K], F32, name="o")
             nc.vector.scalar_tensor_tensor(
-                out=o[:], in0=acc[:], scalar=gain[:, m : m + 1], in1=vs[:, m, :], op0=MULT, op1=SUB
+                out=o[:], in0=banks[m][:], scalar=gain[:, m : m + 1], in1=vs[:, m, :], op0=MULT, op1=SUB
             )
             nc.sync.dma_start(out=out[cols, :], in_=o[:])
 
         with tc.manual_schedule(engines={ENG.PE, ENG.Activation, ENG.DVE}):
-            product(0)
+            widen(0, "V")
+            widen(1, "S")
             turn(0)
-            settle(0)
-            product(1)
             turn(1)
-            settle(1)
-            nc.vector.tensor_copy(out=rt[:].rearrange("p w i -> p (w i)"), in_=rt_in[:].rearrange("p w g t -> p (w g t)"))
+            late(0)
+            widen(2, "S")
+            late(1)
             quant_x(0)
-            product(2)
+            widen(3, "S")
+            turn(2)
+            nc.vector.tensor_copy(out=rt[:].rearrange("p w i -> p (w i)"), in_=rt_in[:].rearrange("p w g t -> p (w g t)"))
             quant_x(1)
-            product(3)
+            late(2)
             for s in range(2 * G):
                 g, h = divmod(s, 2)
-                if s + 1 < 2 * G:
-                    turn(2 * s + 2)
-                    turn(2 * s + 3)
-                    settle(2 * s + 2)
-                    settle(2 * s + 3)
-                wide_pair(2 * s)
-                wide_pair(2 * s + 1)
+                a, b = 2 * s, 2 * s + 1
+                more = s + 2 < 2 * G
+                if s == 0:
+                    for i in (0, 1):
+                        for kind in ("z", "e"):
+                            mm_wide(kind, i)
+                            evac_wide(kind, i)
+                        if i == 0:
+                            turn(3)
+                            late(3)
+                            quant_x(2)
+                            product(4)
+                            quant_x(3)
+                            product(5)
+                    continue
+                if more:
+                    product(2 * s + 4)
+                if s < 2 * G - 1:
+                    turn(a + 2)
+                    turn(b + 2)
+                    settle(a + 2)
+                    settle(b + 2)
+                    quant_x(a + 2)
+                for kind in ("z", "e"):
+                    if s == 2 * G - 1 and kind == "e":
+                        narrow_mm(g - 1, 2 * h)
+                        narrow_mm(g - 1, 2 * h + 1)
+                    mm_wide(kind, a)
+                    mm_wide(kind, b)
+                    evac_wide(kind, a)
+                    evac_wide(kind, b)
+                    if s == 2 * G - 1 and kind == "z":
+                        weave("z", g, 256, 512, "S")
                 if g > 0:
                     weave("z", g - 1, 256 * h, 256 * h + 256, "S")
-                if s >= 4:
-                    weave("e", 0, 128 * (s - 4), 128 * (s - 3), "S")
-                if s + 2 < 2 * G:
-                    product(2 * s + 4)
-                if s + 1 < 2 * G:
-                    quant_x(2 * s + 2)
-                if s + 2 < 2 * G:
+                if more:
                     product(2 * s + 5)
-                if s + 1 < 2 * G:
-                    quant_x(2 * s + 3)
+                if 0 < s < 2 * G - 1:
+                    quant_x(b + 2)
+                if s == 6:
+                    weave("e", 0, 0, 512, "V")
+                    weave("e", 1, 0, 512, "V")
+                    quant_wide("e", 0)
+                if s == 7:
+                    weave("e", 2, 0, 512, "V")
+                    quant_wide("e", 1)
                 if g > 0:
+                    if s < 2 * G - 1:
+                        narrow_mm(g - 1, 2 * h)
+                        narrow_mm(g - 1, 2 * h + 1)
+                    evac_narrow(g - 1, 2 * h)
+                    evac_narrow(g - 1, 2 * h + 1)
                     if h == 0 and g > 1:
                         quant_wide("z", g - 2)
-                    narrow_mm(g - 1, 2 * h)
-                    narrow_mm(g - 1, 2 * h + 1)
                     quant_narrow(g - 1, h)
                 if s == 4:
                     nc.vector.reciprocal(out=ipsi[:], in_=psi_in[:, :, 0])
                     nc.vector.tensor_scalar(out=gain[:], in0=ipsi[:], scalar1=1.0 / N, scalar2=None, op0=MULT)
             g = G - 1
-            weave("z", g, 256, 512, "S")
+            for c in range(4):
+                narrow_mm(g, c)
             weave("z", g, 0, 256, "V")
             quant_wide("z", g - 1)
-            narrow_mm(g, 0)
-            quant_wide("z", g)
-            narrow_mm(g, 1)
             scaled_v(4)
+            evac_narrow(g, 0)
+            quant_wide("z", g)
             scaled_v(5)
-            weave("e", 1, 0, 512, "S")
-            quant_wide("e", 0)
-            quant_narrow(g, 0)
-            narrow_mm(g, 2)
-            narrow_mm(g, 3)
-            weave("e", 2, 0, 512, "V")
-            quant_narrow(g, 1)
-            finish(4)
-            scaled_v(6)
-            scaled_v(7)
             weave("e", 3, 256, 512, "S")
-            finish(5)
-            weave("e", 3, 0, 256, "V")
-            quant_wide("e", 1)
-            finish(6)
+            evac_narrow(g, 1)
+            evac_narrow(g, 2)
+            quant_narrow(g, 0)
+            evac_narrow(g, 3)
             quant_wide("e", 2)
-            quant_wide("e", 3)
-            finish(7)
-            for m in range(4):
+            quant_narrow(g, 1)
+            s2(4, (0, 1, 2))
+            s2(5, (0, 1, 2))
+            s2(4, (3,))
+            s2(5, (3,))
+            weave("e", 3, 0, 256, "V")
+            for m in (6, 7, 0, 1, 2, 3):
                 scaled_v(m)
+            epi(4)
+            s2(6, (0, 1, 2, 3))
+            epi(5)
+            quant_wide("e", 3)
+            s2(7, (0, 1, 2, 3))
+            epi(6)
             for m in range(4):
-                finish(m)
+                s2(m, (0, 1, 2, 3))
+                epi((7, 0, 1, 2)[m])
+            epi(3)

@@ -24,6 +24,7 @@ T = 4
 G = N // (P * T)
 J = D // (P * T)
 HALF = D // 2
+AHEAD = ((), (6, 7, 8), (9, 10, 11), (12, 13), (14, 15), (), (), ())
 
 
 def tile_factoranalysisemloadinggradient_w8_kernel(
@@ -32,7 +33,10 @@ def tile_factoranalysisemloadinggradient_w8_kernel(
     nc = tc.nc
     with ExitStack() as ctx:
         keep = ctx.enter_context(tc.tile_pool(name="keep", bufs=1))
-        work = ctx.enter_context(tc.tile_pool(name="work", bufs=4))
+        work = ctx.enter_context(tc.tile_pool(name="work", bufs=3))
+        xwork = ctx.enter_context(tc.tile_pool(name="xwork", bufs=6))
+        nwork = ctx.enter_context(tc.tile_pool(name="nwork", bufs=2))
+        owork = ctx.enter_context(tc.tile_pool(name="owork", bufs=8))
         xps = ctx.enter_context(tc.psum_pool(name="xps", bufs=2))
         aps = ctx.enter_context(tc.psum_pool(name="aps", bufs=6))
 
@@ -40,6 +44,7 @@ def tile_factoranalysisemloadinggradient_w8_kernel(
         sc = keep.tile([P, D], F32, name="sc")
         scol = keep.tile([P, J, T], F32, name="scol")
         nc.scalar.dma_start(out=scol[:], in_=x_scale.rearrange("o (j p t) -> p (o j) t", p=P, t=T))
+        rt_in = keep.tile([P, 2, G, T], BF16, name="rt_in")
         xb = []
         for s in range(2 * G):
             xb.append(keep.tile([P, 2, D], U8, name="xb%d" % s))
@@ -60,7 +65,6 @@ def tile_factoranalysisemloadinggradient_w8_kernel(
         ps32 = p_scales.bitcast(I32)
         bs32 = beta_scales.bitcast(I32)
         pw = p_words.rearrange("g p n t -> p g (n t)")
-        rt_in = keep.tile([P, 2, G, T], BF16, name="rt_in")
         rt = keep.tile([P, 2, G * T], F32, name="rt")
         psi_in = keep.tile([P, D // P, 2], BF16, name="psi_in")
         v_in = keep.tile([P, D // P, K], BF16, name="v_in")
@@ -73,14 +77,14 @@ def tile_factoranalysisemloadinggradient_w8_kernel(
         nc.sync.dma_start(out=wb[:], in_=beta_words.rearrange("g p n t -> p g (n t)"))
         load_x(1)
         nc.sync.dma_start(out=wp[0][:], in_=pw[:, :, 0 : HALF * T])
+        with nc.allow_non_contiguous_dma(reason="small vectors laid on the partitions"):
+            nc.sync.dma_start(out=rt_in[:, 1, :, :], in_=t.rearrange("(g p t) -> p g t", p=P, t=T))
+            nc.sync.dma_start(out=rt_in[:, 0, :, :], in_=r.rearrange("(g p t) -> p g t", p=P, t=T))
         for q in range(4):
             rows = slice(32 * q, 32 * q + 8)
             nc.sync.dma_start(out=ws[rows, 0:D].bitcast(I32), in_=ps32[:, 4 * q : 4 * q + 4, :])
-        nc.sync.dma_start(out=sc[:], in_=x_scale.rearrange("o k -> (o k)").partition_broadcast(P))
-        with nc.allow_non_contiguous_dma(reason="small vectors laid on the partitions"):
-            nc.gpsimd.dma_start(out=rt_in[:, 1, :, :], in_=t.rearrange("(g p t) -> p g t", p=P, t=T))
-            nc.gpsimd.dma_start(out=rt_in[:, 0, :, :], in_=r.rearrange("(g p t) -> p g t", p=P, t=T))
         load_x(2)
+        nc.sync.dma_start(out=sc[:], in_=x_scale.rearrange("o k -> (o k)").partition_broadcast(P))
         nc.sync.dma_start(out=wp[1][:], in_=pw[:, :, HALF * T : D * T])
         for s in range(3, 2 * G):
             load_x(s)
@@ -92,9 +96,9 @@ def tile_factoranalysisemloadinggradient_w8_kernel(
         gx = {}
         xc = []
         xq = []
-        for i in range(G * T):
-            xc.append(keep.tile([P, J * P], U32, name="xc%d" % i, align_bytes=64))
-            xq.append(keep.tile([P, J * P], U8, name="xq%d" % i, align_bytes=64))
+        for s in range(2 * G):
+            xc.append(keep.tile([P, 2, J * P], U32, name="xc%d" % s, align_bytes=64))
+            xq.append(keep.tile([P, 2, J * P], U8, name="xq%d" % s, align_bytes=64))
         zc, zq, ec, eq = [], [], [], []
         for g in range(G):
             zc.append(keep.tile([P, K], U32, name="zc%d" % g, align_bytes=64))
@@ -104,12 +108,12 @@ def tile_factoranalysisemloadinggradient_w8_kernel(
 
         def product(i):
             s, h = divmod(i, 2)
-            xs[i] = work.tile([P, D], BF16, name="xs")
+            xs[i] = xwork.tile([P, D], BF16, name="xs")
             nc.vector.tensor_tensor(out=xs[i][:], in0=xb[s][:, h, :].bitcast(FP8), in1=sc[:], op=MULT)
 
         def widen(i, eng):
             s, h = divmod(i, 2)
-            xs[i] = work.tile([P, D], BF16, name="xs")
+            xs[i] = xwork.tile([P, D], BF16, name="xs")
             for j in range(J):
                 cols = slice(j * HALF, (j + 1) * HALF)
                 if eng == "V":
@@ -118,10 +122,12 @@ def tile_factoranalysisemloadinggradient_w8_kernel(
                     nc.scalar.copy(out=xs[i][:, cols], in_=xb[s][:, h, cols].bitcast(FP8))
 
         def late(i):
-            gx[i] = work.tile([P, J * P * T], BF16, name="gx", align_bytes=64)
+            s, h = divmod(i, 2)
+            if h == 0:
+                gx[s] = work.tile([P, 2, J * P * T], BF16, name="gx", align_bytes=64)
             for j in range(J):
                 nc.vector.tensor_tensor(
-                    out=gx[i][:, j * P * T : (j + 1) * P * T].rearrange("p (r u e) -> p r u e", u=2, e=2),
+                    out=gx[s][:, h, j * P * T : (j + 1) * P * T].rearrange("p (r u e) -> p r u e", u=2, e=2),
                     in0=turned[i][:, j, :, :].bitcast(BF16).rearrange("p u (r e) -> p r u e", e=2),
                     in1=scol[:, j, :].rearrange("p (u e) -> p u e", e=2).unsqueeze(1).to_broadcast([P, P, 2, 2]),
                     op=MULT,
@@ -141,22 +147,32 @@ def tile_factoranalysisemloadinggradient_w8_kernel(
 
         def settle(i):
             xt = turned[i]
-            gx[i] = work.tile([P, J * P * T], BF16, name="gx", align_bytes=64)
+            s, h = divmod(i, 2)
+            if h == 0:
+                gx[s] = work.tile([P, 2, J * P * T], BF16, name="gx", align_bytes=64)
             nc.scalar.copy(
-                out=gx[i][:].bitcast(F32).rearrange("p (j r u) -> p j r u", j=J, u=2),
+                out=gx[s][:, h, :].bitcast(F32).rearrange("p (j r u) -> p j r u", j=J, u=2),
                 in_=xt[:].rearrange("p j u r -> p j r u"),
             )
 
         def quant_x(i):
-            nc.vector.quantize_mx(out=xc[i][:].bitcast(X4), scales=xq[i][:], in_=gx[i][:])
+            s, h = divmod(i, 2)
+            nc.vector.quantize_mx(out=xc[s][:, h, :].bitcast(X4), scales=xq[s][:, h, :], in_=gx[s][:, h, :])
+
+        def quant_pair(s):
+            nc.vector.quantize_mx(
+                out=xc[s][:].rearrange("p h w -> p (h w)").bitcast(X4),
+                scales=xq[s][:].rearrange("p h w -> p (h w)"),
+                in_=gx[s][:].rearrange("p h w -> p (h w)"),
+            )
 
         def mx(acc, i, w_tile, w_word, s_col, width):
             for j in range(J):
                 cols = slice(j * P, (j + 1) * P)
                 nc.tensor.matmul_mx(
                     out=acc,
-                    lhsT=xc[i][:, cols].bitcast(X4),
-                    lhsT_scale=xq[i][:, cols],
+                    lhsT=xc[i // 2][:, i % 2, cols].bitcast(X4),
+                    lhsT_scale=xq[i // 2][:, i % 2, cols],
                     rhs=w_tile[:, j, w_word * T : (w_word + width) * T].bitcast(X4),
                     rhs_scale=ws[4 * j : P, s_col : s_col + width],
                     start=(j == 0),
@@ -213,21 +229,21 @@ def tile_factoranalysisemloadinggradient_w8_kernel(
 
         def evac_narrow(g, c):
             acc = banks["n", g, c]
-            if c % 2 == 0:
-                narrow[g, c // 2] = work.tile([P, 2, P, T], BF16, name="en", align_bytes=64)
+            if c == 0:
+                narrow[g] = nwork.tile([P, 4, P, T], BF16, name="en", align_bytes=64)
             nc.vector.tensor_tensor(
-                out=narrow[g, c // 2][:, c % 2, :, :],
+                out=narrow[g][:, c, :, :],
                 in0=acc[:].rearrange("p t d -> p d t"),
                 in1=rt[:, 0, g * T : (g + 1) * T].unsqueeze(1).to_broadcast([P, P, T]),
                 op=MULT,
             )
 
-        def quant_narrow(g, h):
-            cols = slice(HALF + 2 * P * h, HALF + 2 * P * (h + 1))
+        def quant_narrow(g, lo, hi):
+            cols = slice(HALF + P * lo, HALF + P * hi)
             nc.vector.quantize_mx(
                 out=ec[g][:, cols].bitcast(X4),
                 scales=eq[g][:, cols],
-                in_=narrow[g, h][:].rearrange("p b d t -> p (b d t)"),
+                in_=narrow[g][:, lo:hi, :, :].rearrange("p b d t -> p (b d t)"),
             )
 
         ipsi = keep.tile([P, D // P], F32, name="ipsi")
@@ -255,7 +271,7 @@ def tile_factoranalysisemloadinggradient_w8_kernel(
 
         def epi(m):
             cols = slice(P * m, P * (m + 1))
-            o = work.tile([P, K], F32, name="o")
+            o = owork.tile([P, K], F32, name="o")
             nc.vector.scalar_tensor_tensor(
                 out=o[:], in0=banks[m][:], scalar=gain[:, m : m + 1], in1=vs[:, m, :], op0=MULT, op1=SUB
             )
@@ -272,94 +288,101 @@ def tile_factoranalysisemloadinggradient_w8_kernel(
             quant_x(0)
             widen(3, "S")
             turn(2)
-            nc.vector.tensor_copy(out=rt[:].rearrange("p w i -> p (w i)"), in_=rt_in[:].rearrange("p w g t -> p (w g t)"))
             quant_x(1)
+            nc.vector.tensor_copy(out=rt[:].rearrange("p w i -> p (w i)"), in_=rt_in[:].rearrange("p w g t -> p (w g t)"))
             late(2)
-            for s in range(2 * G):
+            mm_wide("z", 0)
+            evac_wide("z", 0)
+            turn(3)
+            widen(4, "S")
+            late(3)
+            mm_wide("z", 1)
+            evac_wide("z", 1)
+            widen(5, "S")
+            quant_pair(1)
+            for i in (0, 1):
+                mm_wide("e", i)
+                evac_wide("e", i)
+            for s in range(1, 2 * G):
                 g, h = divmod(s, 2)
                 a, b = 2 * s, 2 * s + 1
-                more = s + 2 < 2 * G
-                if s == 0:
-                    for i in (0, 1):
-                        for kind in ("z", "e"):
-                            mm_wide(kind, i)
-                            evac_wide(kind, i)
-                        if i == 0:
-                            turn(3)
-                            late(3)
-                            quant_x(2)
-                            product(4)
-                            quant_x(3)
-                            product(5)
-                    continue
-                if more:
-                    product(2 * s + 4)
-                if s < 2 * G - 1:
+                if s + 1 < 2 * G:
                     turn(a + 2)
                     turn(b + 2)
-                    settle(a + 2)
-                    settle(b + 2)
-                    quant_x(a + 2)
+                    if s == 1:
+                        late(a + 2)
+                        late(b + 2)
+                    else:
+                        settle(a + 2)
+                        settle(b + 2)
+                for i in AHEAD[s][:2]:
+                    product(i)
                 for kind in ("z", "e"):
                     if s == 2 * G - 1 and kind == "e":
-                        narrow_mm(g - 1, 2 * h)
-                        narrow_mm(g - 1, 2 * h + 1)
+                        narrow_mm(g - 1, 2)
+                        narrow_mm(g - 1, 3)
                     mm_wide(kind, a)
                     mm_wide(kind, b)
                     evac_wide(kind, a)
                     evac_wide(kind, b)
                     if s == 2 * G - 1 and kind == "z":
                         weave("z", g, 256, 512, "S")
-                if g > 0:
-                    weave("z", g - 1, 256 * h, 256 * h + 256, "S")
-                if more:
-                    product(2 * s + 5)
-                if 0 < s < 2 * G - 1:
-                    quant_x(b + 2)
                 if s == 6:
+                    weave("z", 2, 0, 512, "S")
+                elif g > 0 and s < 6:
+                    weave("z", g - 1, 256 * h, 256 * h + 256, "S")
+                if s + 1 < 2 * G:
+                    quant_pair(s + 1)
+                for i in AHEAD[s][2:]:
+                    product(i)
+                if s == 5:
                     weave("e", 0, 0, 512, "V")
+                if s == 6:
                     weave("e", 1, 0, 512, "V")
                     quant_wide("e", 0)
                 if s == 7:
                     weave("e", 2, 0, 512, "V")
-                    quant_wide("e", 1)
+                    quant_wide("z", 2)
                 if g > 0:
-                    if s < 2 * G - 1:
+                    if s + 1 < 2 * G:
                         narrow_mm(g - 1, 2 * h)
                         narrow_mm(g - 1, 2 * h + 1)
                     evac_narrow(g - 1, 2 * h)
                     evac_narrow(g - 1, 2 * h + 1)
                     if h == 0 and g > 1:
                         quant_wide("z", g - 2)
-                    quant_narrow(g - 1, h)
+                        quant_narrow(g - 2, 0, 4)
                 if s == 4:
                     nc.vector.reciprocal(out=ipsi[:], in_=psi_in[:, :, 0])
                     nc.vector.tensor_scalar(out=gain[:], in0=ipsi[:], scalar1=1.0 / N, scalar2=None, op0=MULT)
             g = G - 1
+            s2(4, (0, 1))
             for c in range(4):
                 narrow_mm(g, c)
+            quant_wide("e", 1)
             weave("z", g, 0, 256, "V")
-            quant_wide("z", g - 1)
-            scaled_v(4)
+            quant_narrow(g - 1, 0, 4)
             evac_narrow(g, 0)
             quant_wide("z", g)
+            scaled_v(4)
             scaled_v(5)
             weave("e", 3, 256, 512, "S")
             evac_narrow(g, 1)
             evac_narrow(g, 2)
-            quant_narrow(g, 0)
+            quant_narrow(g, 0, 2)
             evac_narrow(g, 3)
             quant_wide("e", 2)
-            quant_narrow(g, 1)
-            s2(4, (0, 1, 2))
+            quant_narrow(g, 2, 4)
+            s2(4, (2,))
             s2(5, (0, 1, 2))
+            s2(6, (0, 1, 2))
             s2(4, (3,))
             s2(5, (3,))
+            s2(6, (3,))
             weave("e", 3, 0, 256, "V")
             for m in (6, 7, 0, 1, 2, 3):
                 scaled_v(m)
             epi(4)
-            s2(6, (0, 1, 2, 3))
             epi(5)
             quant_wide("e", 3)
             s2(7, (0, 1, 2, 3))

@@ -36,7 +36,7 @@ def tile_factoranalysisemloadinggradient_w8_kernel(
         work = ctx.enter_context(tc.tile_pool(name="work", bufs=3))
         xwork = ctx.enter_context(tc.tile_pool(name="xwork", bufs=6))
         nwork = ctx.enter_context(tc.tile_pool(name="nwork", bufs=2))
-        owork = ctx.enter_context(tc.tile_pool(name="owork", bufs=8))
+        owork = ctx.enter_context(tc.tile_pool(name="owork", bufs=6))
         xps = ctx.enter_context(tc.psum_pool(name="xps", bufs=2))
         aps = ctx.enter_context(tc.psum_pool(name="aps", bufs=6))
 
@@ -46,12 +46,11 @@ def tile_factoranalysisemloadinggradient_w8_kernel(
         nc.scalar.dma_start(out=scol[:], in_=x_scale.rearrange("o (j p t) -> p (o j) t", p=P, t=T))
         rt_in = keep.tile([P, 2, G, T], BF16, name="rt_in")
         xb = []
-        for s in range(2 * G):
-            xb.append(keep.tile([P, 2, D], U8, name="xb%d" % s))
+        for g in range(G):
+            xb.append(keep.tile([P, T, D], U8, name="xb%d" % g))
 
-        def load_x(s):
-            g, h = divmod(s, 2)
-            nc.sync.dma_start(out=xb[s][:], in_=x_in[g][:, 2 * h : 2 * h + 2, :])
+        def load_x(g, lo, hi):
+            nc.sync.dma_start(out=xb[g][:, lo:hi, :], in_=x_in[g][:, lo:hi, :])
 
         ws = keep.tile([P, D + K], U8, name="ws", align_bytes=64)
         nc.vector.memset(ws[:].bitcast(I32), 0)
@@ -69,13 +68,12 @@ def tile_factoranalysisemloadinggradient_w8_kernel(
         psi_in = keep.tile([P, D // P, 2], BF16, name="psi_in")
         v_in = keep.tile([P, D // P, K], BF16, name="v_in")
 
-        for h in range(2):
-            nc.sync.dma_start(out=xb[0][:, h : h + 1, :], in_=x_in[0][:, h : h + 1, :])
+        load_x(0, 0, 1)
+        load_x(0, 1, T)
         for q in range(4):
             rows = slice(32 * q, 32 * q + 8)
             nc.sync.dma_start(out=ws[rows, D : D + K].bitcast(I32), in_=bs32[:, 4 * q : 4 * q + 4, :])
         nc.sync.dma_start(out=wb[:], in_=beta_words.rearrange("g p n t -> p g (n t)"))
-        load_x(1)
         nc.sync.dma_start(out=wp[0][:], in_=pw[:, :, 0 : HALF * T])
         with nc.allow_non_contiguous_dma(reason="small vectors laid on the partitions"):
             nc.sync.dma_start(out=rt_in[:, 1, :, :], in_=t.rearrange("(g p t) -> p g t", p=P, t=T))
@@ -83,11 +81,12 @@ def tile_factoranalysisemloadinggradient_w8_kernel(
         for q in range(4):
             rows = slice(32 * q, 32 * q + 8)
             nc.sync.dma_start(out=ws[rows, 0:D].bitcast(I32), in_=ps32[:, 4 * q : 4 * q + 4, :])
-        load_x(2)
+        load_x(1, 0, 2)
         nc.sync.dma_start(out=sc[:], in_=x_scale.rearrange("o k -> (o k)").partition_broadcast(P))
+        load_x(1, 2, T)
         nc.sync.dma_start(out=wp[1][:], in_=pw[:, :, HALF * T : D * T])
-        for s in range(3, 2 * G):
-            load_x(s)
+        load_x(2, 0, T)
+        load_x(3, 0, T)
         with nc.allow_non_contiguous_dma(reason="small vectors laid on the partitions"):
             nc.sync.dma_start(out=psi_in[:, :, 0:1], in_=psi.rearrange("(m p o) -> p m o", p=P, o=1))
         nc.sync.dma_start(out=v_in[:], in_=v.rearrange("(m p) k -> p m k", p=P))
@@ -107,19 +106,19 @@ def tile_factoranalysisemloadinggradient_w8_kernel(
             eq.append(keep.tile([P, D], U8, name="eq%d" % g, align_bytes=64))
 
         def product(i):
-            s, h = divmod(i, 2)
+            g, ti = divmod(i, T)
             xs[i] = xwork.tile([P, D], BF16, name="xs")
-            nc.vector.tensor_tensor(out=xs[i][:], in0=xb[s][:, h, :].bitcast(FP8), in1=sc[:], op=MULT)
+            nc.vector.tensor_tensor(out=xs[i][:], in0=xb[g][:, ti, :].bitcast(FP8), in1=sc[:], op=MULT)
 
         def widen(i, eng):
-            s, h = divmod(i, 2)
+            g, ti = divmod(i, T)
             xs[i] = xwork.tile([P, D], BF16, name="xs")
             for j in range(J):
                 cols = slice(j * HALF, (j + 1) * HALF)
                 if eng == "V":
-                    nc.vector.tensor_copy(out=xs[i][:, cols], in_=xb[s][:, h, cols].bitcast(FP8))
+                    nc.vector.tensor_copy(out=xs[i][:, cols], in_=xb[g][:, ti, cols].bitcast(FP8))
                 else:
-                    nc.scalar.copy(out=xs[i][:, cols], in_=xb[s][:, h, cols].bitcast(FP8))
+                    nc.scalar.copy(out=xs[i][:, cols], in_=xb[g][:, ti, cols].bitcast(FP8))
 
         def late(i):
             s, h = divmod(i, 2)
@@ -253,29 +252,37 @@ def tile_factoranalysisemloadinggradient_w8_kernel(
         def scaled_v(m):
             nc.scalar.activation(out=vs[:, m, :], in_=v_in[:, m, :], func=COPY, scale=ipsi[:, m : m + 1])
 
-        def s2(m, groups):
-            if m not in banks:
+        def s2(m, groups, lo=0, hi=K):
+            if (m, lo) not in banks:
                 acc_m = aps.tile([P, K], F32, name="acc")
-                banks[m] = acc_m
+                banks[m, lo] = acc_m
             cols = slice(P * m, P * (m + 1))
             for g in groups:
                 nc.tensor.matmul_mx(
-                    out=banks[m][:],
+                    out=banks[m, lo][:, 0 : hi - lo],
                     lhsT=ec[g][:, cols].bitcast(X4),
                     lhsT_scale=eq[g][:, cols],
-                    rhs=zc[g][:].bitcast(X4),
-                    rhs_scale=zq[g][:],
+                    rhs=zc[g][:, lo:hi].bitcast(X4),
+                    rhs_scale=zq[g][:, lo:hi],
                     start=(g == 0),
                     stop=(g == G - 1),
                 )
 
-        def epi(m):
-            cols = slice(P * m, P * (m + 1))
+        def epi(m, lo=0, hi=K):
             o = owork.tile([P, K], F32, name="o")
             nc.vector.scalar_tensor_tensor(
-                out=o[:], in0=banks[m][:], scalar=gain[:, m : m + 1], in1=vs[:, m, :], op0=MULT, op1=SUB
+                out=o[:, lo:hi], in0=banks[m, lo][:, 0 : hi - lo], scalar=gain[:, m : m + 1], in1=vs[:, m, lo:hi], op0=MULT, op1=SUB
             )
-            nc.sync.dma_start(out=out[cols, :], in_=o[:])
+            nc.sync.dma_start(out=out[P * m : P * (m + 1), lo:hi], in_=o[:, lo:hi])
+
+        def epi_late(m):
+            d = owork.tile([P, K], F32, name="d")
+            nc.vector.scalar_tensor_tensor(
+                out=d[:], in0=banks[m, 0][:], scalar=1.0 / N, in1=v_in[:, m, :], op0=MULT, op1=SUB
+            )
+            o = owork.tile([P, K], F32, name="o")
+            nc.scalar.activation(out=o[:], in_=d[:], func=COPY, scale=ipsi[:, m : m + 1])
+            nc.sync.dma_start(out=out[P * m : P * (m + 1), :], in_=o[:])
 
         with tc.manual_schedule(engines={ENG.PE, ENG.Activation, ENG.DVE}):
             widen(0, "V")
@@ -283,20 +290,20 @@ def tile_factoranalysisemloadinggradient_w8_kernel(
             turn(0)
             turn(1)
             late(0)
-            widen(2, "S")
-            late(1)
             quant_x(0)
-            widen(3, "S")
+            widen(2, "S")
+            mm_wide("z", 0)
             turn(2)
+            late(1)
             quant_x(1)
             nc.vector.tensor_copy(out=rt[:].rearrange("p w i -> p (w i)"), in_=rt_in[:].rearrange("p w g t -> p (w g t)"))
+            widen(3, "S")
             late(2)
-            mm_wide("z", 0)
             evac_wide("z", 0)
+            mm_wide("z", 1)
             turn(3)
             widen(4, "S")
             late(3)
-            mm_wide("z", 1)
             evac_wide("z", 1)
             widen(5, "S")
             quant_pair(1)
@@ -331,17 +338,16 @@ def tile_factoranalysisemloadinggradient_w8_kernel(
                     weave("z", 2, 0, 512, "S")
                 elif g > 0 and s < 6:
                     weave("z", g - 1, 256 * h, 256 * h + 256, "S")
-                if s + 1 < 2 * G:
-                    quant_pair(s + 1)
-                for i in AHEAD[s][2:]:
-                    product(i)
                 if s == 5:
                     weave("e", 0, 0, 512, "V")
                 if s == 6:
                     weave("e", 1, 0, 512, "V")
                     quant_wide("e", 0)
+                if s + 1 < 2 * G:
+                    quant_pair(s + 1)
+                for i in AHEAD[s][2:]:
+                    product(i)
                 if s == 7:
-                    weave("e", 2, 0, 512, "V")
                     quant_wide("z", 2)
                 if g > 0:
                     if s + 1 < 2 * G:
@@ -359,14 +365,13 @@ def tile_factoranalysisemloadinggradient_w8_kernel(
             s2(4, (0, 1))
             for c in range(4):
                 narrow_mm(g, c)
-            quant_wide("e", 1)
+            weave("e", 2, 0, 512, "S")
             weave("z", g, 0, 256, "V")
+            quant_wide("e", 1)
             quant_narrow(g - 1, 0, 4)
             evac_narrow(g, 0)
             quant_wide("z", g)
-            scaled_v(4)
-            scaled_v(5)
-            weave("e", 3, 256, 512, "S")
+            weave("e", 3, 0, 512, "S")
             evac_narrow(g, 1)
             evac_narrow(g, 2)
             quant_narrow(g, 0, 2)
@@ -379,15 +384,17 @@ def tile_factoranalysisemloadinggradient_w8_kernel(
             s2(4, (3,))
             s2(5, (3,))
             s2(6, (3,))
-            weave("e", 3, 0, 256, "V")
-            for m in (6, 7, 0, 1, 2, 3):
-                scaled_v(m)
-            epi(4)
-            epi(5)
+            scaled_v(3)
+            epi_late(4)
+            epi_late(5)
             quant_wide("e", 3)
             s2(7, (0, 1, 2, 3))
-            epi(6)
-            for m in range(4):
+            epi_late(6)
+            for m in range(3):
                 s2(m, (0, 1, 2, 3))
-                epi((7, 0, 1, 2)[m])
-            epi(3)
+                epi_late((7, 0, 1)[m])
+            s2(3, (0, 1, 2, 3), 0, 256)
+            epi_late(2)
+            s2(3, (0, 1, 2, 3), 256, 512)
+            epi(3, 0, 256)
+            epi(3, 256, 512)

from contextlib import ExitStack

import concourse.mybir as mybir
from concourse.masks import make_identity

N, D, K = 2048, 1024, 512
FLOPS = 2 * N * D * (D + K) + 2 * N * D * K

F32 = mybir.dt.float32
BF16 = mybir.dt.bfloat16
U32 = mybir.dt.uint32
I32 = mybir.dt.int32
U8 = mybir.dt.uint8
FP8 = mybir.dt.float8_e4m3fn
X4 = mybir.dt.float8_e4m3fn_x4
MULT = mybir.AluOpType.mult
SUB = mybir.AluOpType.subtract
COPY = mybir.ActivationFunctionType.Copy

ENG = mybir.EngineType

P = 128
T = 4
G = N // (P * T)
J = D // (P * T)
HALF = D // 2
AHEAD = ((), (6, 7, 8), (9, 10, 11), (12, 13), (14, 15), (), (), ())


def tile_factoranalysisemloadinggradient_w8_kernel(
    tc, x_bytes, x_scale, p_words, p_scales, beta_words, beta_scales, r, t, v, psi, out
):
    nc = tc.nc
    with ExitStack() as ctx:
        keep = ctx.enter_context(tc.tile_pool(name="keep", bufs=1))
        work = ctx.enter_context(tc.tile_pool(name="work", bufs=3))
        xwork = ctx.enter_context(tc.tile_pool(name="xwork", bufs=6))
        nwork = ctx.enter_context(tc.tile_pool(name="nwork", bufs=2))
        owork = ctx.enter_context(tc.tile_pool(name="owork", bufs=6))
        xps = ctx.enter_context(tc.psum_pool(name="xps", bufs=2))
        aps = ctx.enter_context(tc.psum_pool(name="aps", bufs=6))

        x_in = x_bytes.rearrange("(g p t) k -> g p t k", p=P, t=T)
        sc = keep.tile([P, D], F32, name="sc")
        scol = keep.tile([P, J, T], F32, name="scol")
        nc.scalar.dma_start(out=scol[:], in_=x_scale.rearrange("o (j p t) -> p (o j) t", p=P, t=T))
        rt_in = keep.tile([P, 2, G, T], BF16, name="rt_in")
        xb = []
        for g in range(G):
            xb.append(keep.tile([P, T, D], U8, name="xb%d" % g))

        def load_x(g, lo, hi):
            nc.sync.dma_start(out=xb[g][:, lo:hi, :], in_=x_in[g][:, lo:hi, :])

        ws = keep.tile([P, D + K], U8, name="ws", align_bytes=64)
        nc.vector.memset(ws[:].bitcast(I32), 0)
        ident = keep.tile([P, P], F32, name="ident")
        make_identity(nc, ident[:])

        wb = keep.tile([P, J, K * T], U8, name="wb", align_bytes=64)
        wp = []
        for h in range(2):
            wp.append(keep.tile([P, J, HALF * T], U8, name="wp%d" % h, align_bytes=64))
        ps32 = p_scales.bitcast(I32)
        bs32 = beta_scales.bitcast(I32)
        pw = p_words.rearrange("g p n t -> p g (n t)")
        rt = keep.tile([P, 2, G * T], F32, name="rt")
        psi_in = keep.tile([P, D // P, 2], BF16, name="psi_in")
        v_in = keep.tile([P, D // P, K], BF16, name="v_in")

        load_x(0, 0, 1)
        load_x(0, 1, T)
        for q in range(4):
            rows = slice(32 * q, 32 * q + 8)
            nc.sync.dma_start(out=ws[rows, D : D + K].bitcast(I32), in_=bs32[:, 4 * q : 4 * q + 4, :])
        nc.sync.dma_start(out=wb[:], in_=beta_words.rearrange("g p n t -> p g (n t)"))
        nc.sync.dma_start(out=wp[0][:], in_=pw[:, :, 0 : HALF * T])
        with nc.allow_non_contiguous_dma(reason="small vectors laid on the partitions"):
            nc.sync.dma_start(out=rt_in[:, 1, :, :], in_=t.rearrange("(g p t) -> p g t", p=P, t=T))
            nc.sync.dma_start(out=rt_in[:, 0, :, :], in_=r.rearrange("(g p t) -> p g t", p=P, t=T))
        for q in range(4):
            rows = slice(32 * q, 32 * q + 8)
            nc.sync.dma_start(out=ws[rows, 0:D].bitcast(I32), in_=ps32[:, 4 * q : 4 * q + 4, :])
        load_x(1, 0, 2)
        nc.sync.dma_start(out=sc[:], in_=x_scale.rearrange("o k -> (o k)").partition_broadcast(P))
        load_x(1, 2, T)
        nc.sync.dma_start(out=wp[1][:], in_=pw[:, :, HALF * T : D * T])
        load_x(2, 0, T)
        load_x(3, 0, T)
        with nc.allow_non_contiguous_dma(reason="small vectors laid on the partitions"):
            nc.sync.dma_start(out=psi_in[:, :, 0:1], in_=psi.rearrange("(m p o) -> p m o", p=P, o=1))
        nc.sync.dma_start(out=v_in[:], in_=v.rearrange("(m p) k -> p m k", p=P))

        xs = {}
        gx = {}
        xc = []
        xq = []
        for s in range(2 * G):
            xc.append(keep.tile([P, 2, J * P], U32, name="xc%d" % s, align_bytes=64))
            xq.append(keep.tile([P, 2, J * P], U8, name="xq%d" % s, align_bytes=64))
        zc, zq, ec, eq = [], [], [], []
        for g in range(G):
            zc.append(keep.tile([P, K], U32, name="zc%d" % g, align_bytes=64))
            zq.append(keep.tile([P, K], U8, name="zq%d" % g, align_bytes=64))
            ec.append(keep.tile([P, D], U32, name="ec%d" % g, align_bytes=64))
            eq.append(keep.tile([P, D], U8, name="eq%d" % g, align_bytes=64))

        def product(i):
            g, ti = divmod(i, T)
            xs[i] = xwork.tile([P, D], BF16, name="xs")
            nc.vector.tensor_tensor(out=xs[i][:], in0=xb[g][:, ti, :].bitcast(FP8), in1=sc[:], op=MULT)

        def widen(i, eng):
            g, ti = divmod(i, T)
            xs[i] = xwork.tile([P, D], BF16, name="xs")
            for j in range(J):
                cols = slice(j * HALF, (j + 1) * HALF)
                if eng == "V":
                    nc.vector.tensor_copy(out=xs[i][:, cols], in_=xb[g][:, ti, cols].bitcast(FP8))
                else:
                    nc.scalar.copy(out=xs[i][:, cols], in_=xb[g][:, ti, cols].bitcast(FP8))

        def late(i):
            s, h = divmod(i, 2)
            if h == 0:
                gx[s] = work.tile([P, 2, J * P * T], BF16, name="gx", align_bytes=64)
            for j in range(J):
                nc.vector.tensor_tensor(
                    out=gx[s][:, h, j * P * T : (j + 1) * P * T].rearrange("p (r u e) -> p r u e", u=2, e=2),
                    in0=turned[i][:, j, :, :].bitcast(BF16).rearrange("p u (r e) -> p r u e", e=2),
                    in1=scol[:, j, :].rearrange("p (u e) -> p u e", e=2).unsqueeze(1).to_broadcast([P, P, 2, 2]),
                    op=MULT,
                )

        turned = {}

        def turn(i):
            words = xs[i][:].bitcast(F32)
            xt = xps.tile([P, J, 2, P], F32, name="xt")
            turned[i] = xt
            for j in range(J):
                for u in range(2):
                    nc.tensor.transpose(
                        xt[:, j, u, :], words[:, 256 * j + u : 256 * (j + 1) : 2], ident[:]
                    )

        def settle(i):
            xt = turned[i]
            s, h = divmod(i, 2)
            if h == 0:
                gx[s] = work.tile([P, 2, J * P * T], BF16, name="gx", align_bytes=64)
            nc.scalar.copy(
                out=gx[s][:, h, :].bitcast(F32).rearrange("p (j r u) -> p j r u", j=J, u=2),
                in_=xt[:].rearrange("p j u r -> p j r u"),
            )

        def quant_x(i):
            s, h = divmod(i, 2)
            nc.vector.quantize_mx(out=xc[s][:, h, :].bitcast(X4), scales=xq[s][:, h, :], in_=gx[s][:, h, :])

        def quant_pair(s):
            nc.vector.quantize_mx(
                out=xc[s][:].rearrange("p h w -> p (h w)").bitcast(X4),
                scales=xq[s][:].rearrange("p h w -> p (h w)"),
                in_=gx[s][:].rearrange("p h w -> p (h w)"),
            )

        def mx(acc, i, w_tile, w_word, s_col, width):
            for j in range(J):
                cols = slice(j * P, (j + 1) * P)
                nc.tensor.matmul_mx(
                    out=acc,
                    lhsT=xc[i // 2][:, i % 2, cols].bitcast(X4),
                    lhsT_scale=xq[i // 2][:, i % 2, cols],
                    rhs=w_tile[:, j, w_word * T : (w_word + width) * T].bitcast(X4),
                    rhs_scale=ws[4 * j : P, s_col : s_col + width],
                    start=(j == 0),
                    stop=(j == J - 1),
                )

        planes = {}

        banks = {}

        def mm_wide(kind, i):
            acc = aps.tile([P, K], F32, name="acc")
            banks[kind, i] = acc
            if kind == "z":
                mx(acc[:], i, wb, 0, D, K)
            else:
                mx(acc[:], i, wp[0], 0, 0, HALF)

        def evac_wide(kind, i):
            g, ti = divmod(i, T)
            if ti == 0:
                planes[kind, g] = keep.tile([P, T, K], BF16, name="%sp%d" % (kind, g))
            w = (0, 1)[kind == "z"]
            nc.scalar.activation(
                out=planes[kind, g][:, ti, :], in_=banks[kind, i][:], func=COPY, scale=rt[:, w, i : i + 1]
            )

        def weave(kind, g, lo, hi, eng):
            if (kind, g, "i") not in planes:
                planes[kind, g, "i"] = keep.tile([P, HALF, T], BF16, name="%si%d" % (kind, g), align_bytes=64)
            o = planes[kind, g, "i"][:, lo:hi, :].rearrange("p (c i) t -> p c t i", i=4)
            a = planes[kind, g][:, :, lo:hi].rearrange("p t (c i) -> p c t i", i=4)
            if eng == "V":
                nc.vector.tensor_copy(out=o, in_=a)
            else:
                nc.scalar.copy(out=o, in_=a)

        def quant_wide(kind, g):
            src = planes[kind, g, "i"][:].rearrange("p c t -> p (c t)")
            if kind == "z":
                nc.vector.quantize_mx(out=zc[g][:].bitcast(X4), scales=zq[g][:], in_=src)
            else:
                nc.vector.quantize_mx(
                    out=ec[g][:, 0:HALF].bitcast(X4), scales=eq[g][:, 0:HALF], in_=src
                )

        narrow = {}

        def narrow_mm(g, c):
            acc = aps.tile([P, T, P], F32, name="acc")
            for ti in range(T):
                mx(acc[:, ti, :], g * T + ti, wp[1], P * c, HALF + P * c, P)
            banks["n", g, c] = acc

        def evac_narrow(g, c):
            acc = banks["n", g, c]
            if c == 0:
                narrow[g] = nwork.tile([P, 4, P, T], BF16, name="en", align_bytes=64)
            nc.vector.tensor_tensor(
                out=narrow[g][:, c, :, :],
                in0=acc[:].rearrange("p t d -> p d t"),
                in1=rt[:, 0, g * T : (g + 1) * T].unsqueeze(1).to_broadcast([P, P, T]),
                op=MULT,
            )

        def quant_narrow(g, lo, hi):
            cols = slice(HALF + P * lo, HALF + P * hi)
            nc.vector.quantize_mx(
                out=ec[g][:, cols].bitcast(X4),
                scales=eq[g][:, cols],
                in_=narrow[g][:, lo:hi, :, :].rearrange("p b d t -> p (b d t)"),
            )

        ipsi = keep.tile([P, D // P], F32, name="ipsi")
        gain = keep.tile([P, D // P], F32, name="gain")
        vs = keep.tile([P, D // P, K], F32, name="vs")

        def scaled_v(m):
            nc.scalar.activation(out=vs[:, m, :], in_=v_in[:, m, :], func=COPY, scale=ipsi[:, m : m + 1])

        def s2(m, groups, lo=0, hi=K):
            if (m, lo) not in banks:
                acc_m = aps.tile([P, K], F32, name="acc")
                banks[m, lo] = acc_m
            cols = slice(P * m, P * (m + 1))
            for g in groups:
                nc.tensor.matmul_mx(
                    out=banks[m, lo][:, 0 : hi - lo],
                    lhsT=ec[g][:, cols].bitcast(X4),
                    lhsT_scale=eq[g][:, cols],
                    rhs=zc[g][:, lo:hi].bitcast(X4),
                    rhs_scale=zq[g][:, lo:hi],
                    start=(g == 0),
                    stop=(g == G - 1),
                )

        def epi(m, lo=0, hi=K):
            o = owork.tile([P, K], F32, name="o")
            nc.vector.scalar_tensor_tensor(
                out=o[:, lo:hi], in0=banks[m, lo][:, 0 : hi - lo], scalar=gain[:, m : m + 1], in1=vs[:, m, lo:hi], op0=MULT, op1=SUB
            )
            nc.sync.dma_start(out=out[P * m : P * (m + 1), lo:hi], in_=o[:, lo:hi])

        def epi_late(m):
            d = owork.tile([P, K], F32, name="d")
            nc.vector.scalar_tensor_tensor(
                out=d[:], in0=banks[m, 0][:], scalar=1.0 / N, in1=v_in[:, m, :], op0=MULT, op1=SUB
            )
            o = owork.tile([P, K], F32, name="o")
            nc.scalar.activation(out=o[:], in_=d[:], func=COPY, scale=ipsi[:, m : m + 1])
            nc.sync.dma_start(out=out[P * m : P * (m + 1), :], in_=o[:])

        with tc.manual_schedule(engines={ENG.PE, ENG.Activation, ENG.DVE}):
            widen(0, "V")
            widen(1, "S")
            turn(0)
            turn(1)
            late(0)
            quant_x(0)
            widen(2, "S")
            mm_wide("z", 0)
            turn(2)
            late(1)
            quant_x(1)
            nc.vector.tensor_copy(out=rt[:].rearrange("p w i -> p (w i)"), in_=rt_in[:].rearrange("p w g t -> p (w g t)"))
            widen(3, "S")
            late(2)
            evac_wide("z", 0)
            mm_wide("z", 1)
            turn(3)
            widen(4, "S")
            late(3)
            evac_wide("z", 1)
            widen(5, "S")
            quant_pair(1)
            for i in (0, 1):
                mm_wide("e", i)
                evac_wide("e", i)
            for s in range(1, 2 * G):
                g, h = divmod(s, 2)
                a, b = 2 * s, 2 * s + 1
                if s + 1 < 2 * G:
                    turn(a + 2)
                    turn(b + 2)
                    if s == 1:
                        late(a + 2)
                        late(b + 2)
                    else:
                        settle(a + 2)
                        settle(b + 2)
                for i in AHEAD[s][:2]:
                    product(i)
                for kind in ("z", "e"):
                    if s == 2 * G - 1 and kind == "e":
                        narrow_mm(g - 1, 2)
                        narrow_mm(g - 1, 3)
                    mm_wide(kind, a)
                    mm_wide(kind, b)
                    evac_wide(kind, a)
                    evac_wide(kind, b)
                    if s == 2 * G - 1 and kind == "z":
                        weave("z", g, 256, 512, "S")
                if s == 6:
                    weave("z", 2, 0, 512, "S")
                elif g > 0 and s < 6:
                    weave("z", g - 1, 256 * h, 256 * h + 256, "S")
                if s == 5:
                    weave("e", 0, 0, 512, "V")
                if s == 6:
                    weave("e", 1, 0, 512, "V")
                    quant_wide("e", 0)
                if s + 1 < 2 * G:
                    quant_pair(s + 1)
                for i in AHEAD[s][2:]:
                    product(i)
                if s == 7:
                    quant_wide("z", 2)
                if g > 0:
                    if s + 1 < 2 * G:
                        narrow_mm(g - 1, 2 * h)
                        narrow_mm(g - 1, 2 * h + 1)
                    evac_narrow(g - 1, 2 * h)
                    evac_narrow(g - 1, 2 * h + 1)
                    if h == 0 and g > 1:
                        quant_wide("z", g - 2)
                        quant_narrow(g - 2, 0, 4)
                if s == 4:
                    nc.vector.reciprocal(out=ipsi[:], in_=psi_in[:, :, 0])
                    nc.vector.tensor_scalar(out=gain[:], in0=ipsi[:], scalar1=1.0 / N, scalar2=None, op0=MULT)
            g = G - 1
            s2(4, (0, 1))
            for c in range(4):
                narrow_mm(g, c)
            weave("e", 2, 0, 512, "S")
            weave("z", g, 0, 256, "V")
            quant_wide("e", 1)
            quant_narrow(g - 1, 0, 4)
            evac_narrow(g, 0)
            quant_wide("z", g)
            weave("e", 3, 0, 512, "S")
            evac_narrow(g, 1)
            evac_narrow(g, 2)
            quant_narrow(g, 0, 2)
            evac_narrow(g, 3)
            quant_wide("e", 2)
            quant_narrow(g, 2, 4)
            s2(4, (2,))
            s2(5, (0, 1, 2))
            s2(6, (0, 1, 2))
            s2(4, (3,))
            s2(5, (3,))
            s2(6, (3,))
            scaled_v(3)
            epi_late(4)
            epi_late(5)
            quant_wide("e", 3)
            s2(7, (0, 1, 2, 3))
            epi_late(6)
            for m in range(3):
                s2(m, (0, 1, 2, 3))
                epi_late((7, 0, 1)[m])
            s2(3, (0, 1, 2, 3), 0, 256)
            epi_late(2)
            s2(3, (0, 1, 2, 3), 256, 512)
            epi(3, 0, 256)
            epi(3, 256, 512)
